import numpy as np
import ml_dtypes


def mxq(x, axis, fmt="e4m3"):
    dtype, down = {"e4m3": (ml_dtypes.float8_e4m3fn, 7), "e5m2": (ml_dtypes.float8_e5m2, 14)}[fmt]
    v = np.moveaxis(np.asarray(x, np.float32).astype(ml_dtypes.bfloat16).astype(np.float64), axis, -1)
    blocks = v.reshape(v.shape[:-1] + (-1, 32))
    amax = np.abs(blocks).max(-1, keepdims=True)
    byte = np.maximum(np.where(amax > 0, np.frexp(amax)[1] - 1 + 127, 0) - down, 1)
    scale = np.exp2(byte - 127.0)
    codes = (blocks / scale).astype(np.float32).astype(dtype).astype(np.float64)
    return np.moveaxis((codes * scale).reshape(v.shape), -1, axis)


WIDE = False


def mx_kscale(k):
    if not WIDE:
        return np.ones(k)
    levels = np.array([10, -10, 5, -5, 0])
    if k % 512:
        return np.exp2(np.random.permutation(np.resize(levels, k // 32))).repeat(32)
    a = np.empty((k // 512, 16))
    for p in range(k // 512):
        a[p, :8] = np.random.permutation(np.resize(levels, 8))
        for g in range(8):
            far = levels[np.abs(levels - a[p, g]) >= 10]
            a[p, g + 8] = far[np.random.randint(len(far))]
    return np.exp2(a.ravel()).repeat(32)


def f64(x):
    return np.asarray(x).astype(np.float64)


def striped(idx):
    return np.tile(np.asarray(idx).reshape(-1, 16).T, (8, 1)).astype(np.uint16)


def unstriped(offs):
    return offs[:16].T.reshape(-1).astype(np.int64)


E2M1 = np.array([0.0, 0.5, 1.0, 1.5, 2.0, 3.0, 4.0, 6.0, -0.0, -0.5, -1.0, -1.5, -2.0, -3.0, -4.0, -6.0])


def pack_weight(w, fmt):
    k, n = w.shape
    w = f64(np.asarray(w, np.float32).astype(ml_dtypes.bfloat16)).reshape(k // 32, 32, n)
    amax = np.abs(w).max(1)
    if fmt == "e4m3":
        byte = np.frexp(amax)[1] - 1 + 127 - 7
    else:
        mant, ex = np.frexp(amax / 6.0)
        byte = np.where(mant > 0.5, ex, ex - 1) + 127
    byte = np.clip(np.where(amax > 0, byte, 1), 1, 254)
    scaled = (w * np.exp2(127.0 - byte)[:, None, :]).reshape(k, n).astype(np.float32)
    by_word = np.ascontiguousarray(scaled.reshape(k // 512, 128, 4, n).transpose(0, 1, 3, 2))
    if fmt == "e4m3":
        words = by_word.astype(ml_dtypes.float8_e4m3fn).view(np.uint8)
    else:
        c = by_word.astype(ml_dtypes.float4_e2m1fn).view(np.uint8) & 0xF
        words = (c[..., 0::2] | (c[..., 1::2] << 4)).reshape(k // 512, 128, 2 * n)
    return np.ascontiguousarray(words), np.ascontiguousarray(byte.astype(np.uint8).reshape(k // 512, 16, n))


def unpack_weight(words, scales, fmt):
    g, _, n = scales.shape
    words = np.ascontiguousarray(words).reshape(g, 128, n, -1)
    if fmt == "e4m3":
        vals = words.view(ml_dtypes.float8_e4m3fn).astype(np.float64)
    else:
        nib = np.empty((g, 128, n, 4), np.uint8)
        nib[..., 0::2] = words & 0xF
        nib[..., 1::2] = words >> 4
        vals = E2M1[nib]
    vals = vals * np.repeat(np.exp2(scales.astype(np.float64) - 127.0), 8, axis=1)[..., None]
    return vals.transpose(0, 1, 3, 2).reshape(g * 512, n)


def silu(v):
    return v / (1.0 + np.exp(-v))


def bf(x):
    return np.asarray(x, np.float32).astype(ml_dtypes.bfloat16)


def planes(Y):
    r, m = Y.shape
    b = f64(bf(Y)).reshape(r // 32, 32, m)
    amax = np.abs(b).max(1)
    byte = np.clip(np.where(amax > 0, np.frexp(amax)[1] - 1 + 127 - 7, 1), 1, 254)
    codes = (b * np.exp2(127.0 - byte)[:, None, :]).reshape(r, m).astype(np.float32).astype(ml_dtypes.float8_e4m3fn).view(np.uint8)
    words = codes.reshape(r // 512, 128, 4, m).transpose(0, 1, 3, 2)
    return np.ascontiguousarray(words), np.ascontiguousarray(byte.astype(np.uint8).reshape(r // 512, 16, m))


B, N, T, D, NQ = 1, 512, 2048, 1024, 512


def setup_inputs():
    n = np.random.standard_normal
    pages = np.random.permutation(T // 64)[:B * N // 64]
    idx = (pages[:, None] * 64 + np.arange(64)[None, :]).reshape(-1)
    s = mx_kscale(D)[:, None]
    kp = pack_weight(n((D, T)) / s, "e2m1")
    return {
        "qT": (n((B, D, NQ)) * s * (1.00 / np.sqrt(D))).astype(np.float32),
        "k_words": np.ascontiguousarray(kp[0].reshape(1, 2, 128, T, 2).transpose(0, 2, 3, 1, 4)).reshape(1, 128, T, 4),
        "k_scales": kp[1],
        "nb": np.tile(0.5 * n(2048), (128, 1)).astype(np.float32),
        "offs": striped(idx),
    }


def reference(qT, k_words, k_scales, nb, offs):
    idx = unstriped(offs)
    pick = lambda x, which: x[:, which].reshape(x.shape[0], B, -1).transpose(1, 0, 2)
    k = unpack_weight(k_words.reshape(1, 128, T, 2, 2).transpose(0, 3, 1, 2, 4).reshape(2, 128, 2 * T), k_scales, "e2m1")
    kg = pick(k, idx)
    qq = mxq(f64(qT), 1, "e4m3")
    a = kg.transpose(0, 2, 1) @ qq
    y = silu(a + pick(f64(nb), idx)[:, :1, :].transpose(0, 2, 1))
    Y = y[0]
    words, scales = planes(Y)
    return Y, words, scales

@@ -1,0 +1,190 @@
+from contextlib import ExitStack
+
+import concourse.mybir as mybir
+from concourse.masks import make_identity
+
+F32 = mybir.dt.float32
+BF16 = mybir.dt.bfloat16
+I32 = mybir.dt.int32
+U32 = mybir.dt.uint32
+U16 = mybir.dt.uint16
+U8 = mybir.dt.uint8
+FP8X4 = mybir.dt.float8_e4m3fn_x4
+FP4X4 = mybir.dt.float4_e2m1fn_x4
+SILU = mybir.ActivationFunctionType.Silu
+
+P = 128
+PACK = 4
+PASSES = 2
+SLOTS = 512
+POOL = 2048
+QUERIES = 512
+CHUNK = 128
+CHUNKS = QUERIES // CHUNK
+QUAD = 32
+LIVE = 3 * QUAD + PACK
+FLOPS = 2 * SLOTS * PASSES * P * PACK * QUERIES
+
+
+def tile_attend_plh_bsilu_kernel(tc, qT, k_words, k_scales, nb, offs, out_0, out_1, out_2):
+    nc = tc.nc
+    with ExitStack() as ctx:
+        keep = ctx.enter_context(tc.tile_pool(name="keep", bufs=1))
+        psum = ctx.enter_context(tc.psum_pool(name="psum", bufs=1))
+
+        offsets = keep.tile([P, SLOTS // 16], U16, name="offsets")
+        nc.sync.dma_start(offsets[:], offs)
+
+        bias_window = keep.tile([P, POOL], F32, name="bias_window", tag="slot1", align_bytes=64)
+        nc.sync.dma_start(out=bias_window[P - 1 : P, :], in_=nb[0:1, :])
+        q_rows = qT[0].rearrange("(o p j) q -> p j o q", o=PASSES, j=PACK)
+        raws = {}
+
+        def load_queries(c):
+            raw = keep.tile([P, PACK, PASSES, CHUNK], F32, name="raw%d" % c, tag="slot%d" % c, align_bytes=64)
+            nc.sync.dma_start(out=raw[:], in_=q_rows[:, :, :, c * CHUNK : (c + 1) * CHUNK])
+            for o in range(PASSES):
+                raws[c, o] = raw[:, :, o, :]
+
+        def load_last_queries(o):
+            c = CHUNKS - 1
+            raw = keep.tile([P, PACK, CHUNK], F32, name="last_raw%d" % o, tag="slot%d" % (c + o), align_bytes=64)
+            nc.sync.dma_start(out=raw[:], in_=q_rows[:, :, o, c * CHUNK : (c + 1) * CHUNK])
+            raws[c, o] = raw[:]
+
+        load_queries(0)
+        word_window = keep.tile([P, POOL], U32, name="word_window", tag="slot3", align_bytes=64)
+        nc.sync.dma_start(
+            out=word_window[:].bitcast(I32),
+            in_=k_words[0].rearrange("p t b -> p (t b)").bitcast(I32),
+        )
+        scale_window = keep.tile([P, POOL], U8, name="scale_window", tag="slot4", align_bytes=64)
+        nc.gpsimd.memset(scale_window[:].bitcast(I32), 0)
+        for quad in range(4):
+            nc.scalar.dma_start(
+                out=scale_window[QUAD * quad : QUAD * quad + PASSES * PACK, :].bitcast(I32),
+                in_=k_scales[:, PACK * quad : PACK * (quad + 1), :].bitcast(I32),
+            )
+        nc.vector.memset(bias_window[0 : P - 1, :], 0.0)
+        second_plane = keep.tile([P, SLOTS], U8, name="second_plane", align_bytes=64)
+        nc.vector.memset(second_plane[:].bitcast(I32), 0)
+        warm_in = keep.tile([P, 8], F32, name="warm_in")
+        warm_out = keep.tile([P, 8], F32, name="warm_out")
+        nc.vector.memset(warm_in[:], 0.0)
+        nc.scalar.activation(warm_out[:], warm_in[:], SILU)
+        identity = keep.tile([P, P], F32, name="identity")
+        make_identity(nc, identity[:])
+
+        bias_listed = keep.tile([P, SLOTS], F32, name="bias_listed", align_bytes=64)
+        nc.vector.tensor_copy(bias_listed[:], bias_window[:].indirect(offsets[:]))
+        load_queries(1)
+        bias_turned = psum.tile([P, PACK, P], F32, name="bias_turned")
+        for u in range(PACK):
+            nc.tensor.transpose(bias_turned[:, u, :], bias_listed[:, u:SLOTS:PACK], identity[:])
+        bias = keep.tile([P, PACK], F32, name="bias")
+        nc.scalar.copy(bias[:], bias_turned[:, :, P - 1])
+
+        scales_listed = keep.tile([P, SLOTS], U8, name="scales_listed", tag="slot2", align_bytes=64)
+        nc.vector.tensor_copy(scales_listed[:], scale_window[:].indirect(offsets[:]))
+        scales_dealt = keep.tile([P, SLOTS], U8, name="scales_dealt", align_bytes=64)
+        nc.vector.tensor_copy(
+            scales_dealt[:].rearrange("p (u h l) -> p h u l", u=PACK, l=4),
+            scales_listed[:].rearrange("p (h l u) -> p h u l", u=PACK, l=4),
+        )
+        nc.sync.dma_start(
+            out=second_plane[0:LIVE, :].bitcast(I32),
+            in_=scales_dealt[PACK : PACK + LIVE, :].bitcast(I32),
+        )
+        load_queries(2)
+        k_planes = [scales_dealt, second_plane]
+
+        words_listed = keep.tile([P, SLOTS], U32, name="words_listed", tag="slot4", align_bytes=64)
+        nc.vector.tensor_copy(words_listed[:], word_window[:].indirect(offsets[:]))
+        load_last_queries(0)
+        k_codes = keep.tile([P, PASSES * SLOTS * 2], U8, name="k_codes", align_bytes=64)
+        nc.vector.tensor_copy(
+            k_codes[:].bitcast(U16).rearrange("p (o u h l) -> p o h u l", o=PASSES, u=PACK, l=2),
+            words_listed[:].bitcast(U16).rearrange("p (h l u o) -> p o h u l", o=PASSES, u=PACK, l=2),
+        )
+        load_last_queries(1)
+
+        y_codes = keep.tile([P, QUERIES], U32, name="y_codes", align_bytes=64)
+        y_plane = keep.tile([P, QUERIES], U8, name="y_plane", align_bytes=64)
+        out_rows = out_0.rearrange("(p u) q -> p u q", u=PACK)
+        out_words = out_1[0].rearrange("p q b -> p (q b)").bitcast(I32)
+
+        def quantise_queries(c):
+            grouped = [
+                keep.tile([P, CHUNK, PACK], BF16, name="grouped%d_%d" % (c, o), align_bytes=64) for o in range(PASSES)
+            ]
+            for o in range(PASSES):
+                source = raws[c, o].rearrange("p j (g i) -> p g j i", i=4)
+                target = grouped[o][:].rearrange("p (g i) j -> p g j i", i=4)
+                if o == 0 or c == 0:
+                    nc.scalar.copy(target, source)
+                else:
+                    nc.vector.tensor_copy(target, source)
+            codes = keep.tile([P, PASSES, CHUNK], U32, name="q_codes%d" % c, align_bytes=64)
+            plane = keep.tile([P, PASSES, CHUNK], U8, name="q_plane%d" % c, align_bytes=64)
+            for o in range(PASSES):
+                nc.vector.quantize_mx(
+                    out=codes[:, o, :].bitcast(FP8X4),
+                    scales=plane[:, o, :],
+                    in_=grouped[o][:].rearrange("p q j -> p (q j)"),
+                )
+            return codes, plane
+
+        def multiply(c, codes, plane):
+            if c < CHUNKS - 1:
+                bank = psum.tile([P, PACK, CHUNK], F32, name="acc%d" % c)
+                acc = [bank[:, u, :] for u in range(PACK)]
+                order = [(u, o) for u in range(PACK) for o in range(PASSES)]
+            else:
+                acc = [psum.tile([P, CHUNK], F32, name="last_acc%d" % u)[:] for u in range(PACK)]
+                order = [(u, o) for o in range(PASSES) for u in range(PACK)]
+            for u, o in order:
+                if True:
+                    column = (o * PACK + u) * P
+                    nc.tensor.matmul_mx(
+                        out=acc[u],
+                        lhsT=k_codes[:, 2 * column : 2 * (column + P)].bitcast(FP4X4),
+                        lhsT_scale=k_planes[o][:, u * P : (u + 1) * P],
+                        rhs=codes[:, o, :].bitcast(FP8X4),
+                        rhs_scale=plane[:, o, :],
+                        start=(o == 0),
+                        stop=(o == PASSES - 1),
+                    )
+            return acc
+
+        def finish(c, acc):
+            cols = slice(c * CHUNK, (c + 1) * CHUNK)
+            y = keep.tile([P, PACK, CHUNK], F32, name="y%d" % c)
+            for u in range(PACK):
+                nc.scalar.activation(y[:, u, :], acc[u], SILU, bias=bias[:, u : u + 1])
+            nc.sync.dma_start(out=out_rows[:, :, cols], in_=y[:])
+            y_grouped = keep.tile([P, CHUNK, PACK], BF16, name="y_grouped%d" % c, align_bytes=64)
+            nc.vector.tensor_copy(
+                y_grouped[:].rearrange("p (g i) u -> p g u i", i=4), y[:].rearrange("p u (g i) -> p g u i", i=4)
+            )
+            nc.vector.quantize_mx(
+                out=y_codes[:, cols].bitcast(FP8X4),
+                scales=y_plane[:, cols],
+                in_=y_grouped[:].rearrange("p q u -> p (q u)"),
+            )
+
+        accs = {}
+        for step in range(CHUNKS + 1):
+            if step < CHUNKS:
+                accs[step] = multiply(step, *quantise_queries(step))
+            if step >= 1:
+                finish(step - 1, accs[step - 1])
+            if step >= CHUNKS - 1:
+                cols = slice(0, step * CHUNK) if step < CHUNKS else slice((step - 1) * CHUNK, QUERIES)
+                nc.sync.dma_start(out=out_words[:, cols], in_=y_codes[:, cols].bitcast(I32))
+
+        for quad in range(4):
+            queue = nc.scalar if quad % 2 == 0 else nc.sync
+            queue.dma_start(
+                out=out_2[0, PACK * quad : PACK * (quad + 1), :].bitcast(I32),
+                in_=y_plane[QUAD * quad : QUAD * quad + PACK, :].bitcast(I32),
+            )

@@ -41,50 +41,47 @@ def tile_attend_plh_bsilu_kernel(tc, qT, k_words, k_scales, nb, offs, out_0, out
         raws = {}
 
         def load_queries(c):
-            raw = keep.tile([P, PACK, PASSES, CHUNK], F32, name="raw%d" % c, tag="slot%d" % c, align_bytes=64)
+            raw = keep.tile([P, PACK, PASSES, CHUNK], F32, name="raw%d" % c, tag="slot%d" % (0, 1, 0, 3)[c], align_bytes=64)
             nc.sync.dma_start(out=raw[:], in_=q_rows[:, :, :, c * CHUNK : (c + 1) * CHUNK])
-            for o in range(PASSES):
-                raws[c, o] = raw[:, :, o, :]
-
-        def load_last_queries(o):
-            c = CHUNKS - 1
-            raw = keep.tile([P, PACK, CHUNK], F32, name="last_raw%d" % o, tag="slot%d" % (c + o), align_bytes=64)
-            nc.sync.dma_start(out=raw[:], in_=q_rows[:, :, o, c * CHUNK : (c + 1) * CHUNK])
-            raws[c, o] = raw[:]
+            raws[c] = raw
 
         load_queries(0)
-        word_window = keep.tile([P, POOL], U32, name="word_window", tag="slot3", align_bytes=64)
+        scale_window = keep.tile([P, POOL], U8, name="scale_window", tag="slot6", align_bytes=64)
+        nc.gpsimd.memset(scale_window[:].bitcast(I32), 0)
+        for quad in range(4):
+            nc.sync.dma_start(
+                out=scale_window[QUAD * quad : QUAD * quad + PASSES * PACK, :].bitcast(I32),
+                in_=k_scales[:, PACK * quad : PACK * (quad + 1), :].bitcast(I32),
+            )
+        seed = keep.tile([P, 8], F32, name="seed", tag="slot4", align_bytes=64)
+        nc.gpsimd.memset(seed[:], 0.0)
+        warm_in = keep.tile([P, 8], BF16, name="warm_in")
+        nc.vector.tensor_copy(warm_in[:], seed[:])
+        warm_out = keep.tile([P, 8], F32, name="warm_out")
+        nc.scalar.activation(warm_out[:], warm_in[:], SILU)
+        word_window = keep.tile([P, POOL], U32, name="word_window", tag="slot4", align_bytes=64)
         nc.sync.dma_start(
             out=word_window[:].bitcast(I32),
             in_=k_words[0].rearrange("p t b -> p (t b)").bitcast(I32),
         )
-        scale_window = keep.tile([P, POOL], U8, name="scale_window", tag="slot4", align_bytes=64)
-        nc.gpsimd.memset(scale_window[:].bitcast(I32), 0)
-        for quad in range(4):
-            nc.scalar.dma_start(
-                out=scale_window[QUAD * quad : QUAD * quad + PASSES * PACK, :].bitcast(I32),
-                in_=k_scales[:, PACK * quad : PACK * (quad + 1), :].bitcast(I32),
-            )
-        nc.vector.memset(bias_window[0 : P - 1, :], 0.0)
+        for start, stop in ((0, 383), (383, 768), (768, 959), (959, 1152)):
+            nc.vector.memset(bias_window[0 : P - 1, start:stop], 0.0)
+        nc.gpsimd.memset(bias_window[0 : P - 1, 1152:POOL], 0.0)
         second_plane = keep.tile([P, SLOTS], U8, name="second_plane", align_bytes=64)
         nc.vector.memset(second_plane[:].bitcast(I32), 0)
-        warm_in = keep.tile([P, 8], F32, name="warm_in")
-        warm_out = keep.tile([P, 8], F32, name="warm_out")
-        nc.vector.memset(warm_in[:], 0.0)
-        nc.scalar.activation(warm_out[:], warm_in[:], SILU)
         identity = keep.tile([P, P], F32, name="identity")
         make_identity(nc, identity[:])
 
         bias_listed = keep.tile([P, SLOTS], F32, name="bias_listed", align_bytes=64)
         nc.vector.tensor_copy(bias_listed[:], bias_window[:].indirect(offsets[:]))
         load_queries(1)
-        bias_turned = psum.tile([P, PACK, P], F32, name="bias_turned")
+        bias_turned = psum.tile([P, PACK, P], F32, name="bias_turned", tag="bank7")
         for u in range(PACK):
             nc.tensor.transpose(bias_turned[:, u, :], bias_listed[:, u:SLOTS:PACK], identity[:])
         bias = keep.tile([P, PACK], F32, name="bias")
         nc.scalar.copy(bias[:], bias_turned[:, :, P - 1])
 
-        scales_listed = keep.tile([P, SLOTS], U8, name="scales_listed", tag="slot2", align_bytes=64)
+        scales_listed = keep.tile([P, SLOTS], U8, name="scales_listed", align_bytes=64)
         nc.vector.tensor_copy(scales_listed[:], scale_window[:].indirect(offsets[:]))
         scales_dealt = keep.tile([P, SLOTS], U8, name="scales_dealt", align_bytes=64)
         nc.vector.tensor_copy(
@@ -95,18 +92,15 @@ def tile_attend_plh_bsilu_kernel(tc, qT, k_words, k_scales, nb, offs, out_0, out
             out=second_plane[0:LIVE, :].bitcast(I32),
             in_=scales_dealt[PACK : PACK + LIVE, :].bitcast(I32),
         )
-        load_queries(2)
         k_planes = [scales_dealt, second_plane]
 
-        words_listed = keep.tile([P, SLOTS], U32, name="words_listed", tag="slot4", align_bytes=64)
+        words_listed = keep.tile([P, SLOTS], U32, name="words_listed", tag="slot7", align_bytes=64)
         nc.vector.tensor_copy(words_listed[:], word_window[:].indirect(offsets[:]))
-        load_last_queries(0)
         k_codes = keep.tile([P, PASSES * SLOTS * 2], U8, name="k_codes", align_bytes=64)
         nc.vector.tensor_copy(
             k_codes[:].bitcast(U16).rearrange("p (o u h l) -> p o h u l", o=PASSES, u=PACK, l=2),
             words_listed[:].bitcast(U16).rearrange("p (h l u o) -> p o h u l", o=PASSES, u=PACK, l=2),
         )
-        load_last_queries(1)
 
         y_codes = keep.tile([P, QUERIES], U32, name="y_codes", align_bytes=64)
         y_plane = keep.tile([P, QUERIES], U8, name="y_plane", align_bytes=64)
@@ -114,34 +108,39 @@ def tile_attend_plh_bsilu_kernel(tc, qT, k_words, k_scales, nb, offs, out_0, out
         out_words = out_1[0].rearrange("p q b -> p (q b)").bitcast(I32)
 
         def quantise_queries(c):
-            grouped = [
-                keep.tile([P, CHUNK, PACK], BF16, name="grouped%d_%d" % (c, o), align_bytes=64) for o in range(PASSES)
-            ]
-            for o in range(PASSES):
-                source = raws[c, o].rearrange("p j (g i) -> p g j i", i=4)
-                target = grouped[o][:].rearrange("p (g i) j -> p g j i", i=4)
-                if o == 0 or c == 0:
-                    nc.scalar.copy(target, source)
-                else:
-                    nc.vector.tensor_copy(target, source)
-            codes = keep.tile([P, PASSES, CHUNK], U32, name="q_codes%d" % c, align_bytes=64)
+            grouped = keep.tile(
+                [P, PASSES, CHUNK, PACK], BF16, name="grouped%d" % c, tag="slot%d" % (3, 5, 4, 5)[c], align_bytes=64
+            )
+            source = raws[c][:].rearrange("p j o (g i) -> p o g j i", i=4)
+            target = grouped[:].rearrange("p o (g i) j -> p o g j i", i=4)
+            if c < 2:
+                nc.scalar.copy(target, source)
+            elif c == 2:
+                nc.scalar.copy(target[:, 0], source[:, 0])
+                nc.vector.tensor_copy(target[:, 1], source[:, 1])
+            else:
+                nc.vector.tensor_copy(target, source)
+            codes = keep.tile([P, PASSES, CHUNK], U32, name="q_codes%d" % c, tag="slot%d" % (6, 7, 8, 9)[c], align_bytes=64)
             plane = keep.tile([P, PASSES, CHUNK], U8, name="q_plane%d" % c, align_bytes=64)
-            for o in range(PASSES):
-                nc.vector.quantize_mx(
-                    out=codes[:, o, :].bitcast(FP8X4),
-                    scales=plane[:, o, :],
-                    in_=grouped[o][:].rearrange("p q j -> p (q j)"),
-                )
+            nc.vector.quantize_mx(
+                out=codes[:].rearrange("p o q -> p (o q)").bitcast(FP8X4),
+                scales=plane[:].rearrange("p o q -> p (o q)"),
+                in_=grouped[:].rearrange("p o q j -> p (o q j)"),
+            )
             return codes, plane
 
         def multiply(c, codes, plane):
-            if c < CHUNKS - 1:
-                bank = psum.tile([P, PACK, CHUNK], F32, name="acc%d" % c)
-                acc = [bank[:, u, :] for u in range(PACK)]
-                order = [(u, o) for u in range(PACK) for o in range(PASSES)]
+            banks = (4, 1, 1, 2)[c]
+            first = (0, 4, 5, 6)[c]
+            share = PACK // banks
+            tiles = [
+                psum.tile([P, share, CHUNK], F32, name="acc%d_%d" % (c, b), tag="bank%d" % (first + b)) for b in range(banks)
+            ]
+            acc = [tiles[u // share][:, u % share, :] for u in range(PACK)]
+            if c == 0:
+                order = [(u, o) for o in (0, 1) for u in range(PACK)]
             else:
-                acc = [psum.tile([P, CHUNK], F32, name="last_acc%d" % u)[:] for u in range(PACK)]
-                order = [(u, o) for o in range(PASSES) for u in range(PACK)]
+                order = [(u, o) for u in range(PACK) for o in (1, 0)]
             for u, o in order:
                 if True:
                     column = (o * PACK + u) * P
@@ -151,20 +150,22 @@ def tile_attend_plh_bsilu_kernel(tc, qT, k_words, k_scales, nb, offs, out_0, out
                         lhsT_scale=k_planes[o][:, u * P : (u + 1) * P],
                         rhs=codes[:, o, :].bitcast(FP8X4),
                         rhs_scale=plane[:, o, :],
-                        start=(o == 0),
-                        stop=(o == PASSES - 1),
+                        start=(o == order[0][1]),
+                        stop=(o != order[0][1]),
                     )
             return acc
 
-        def finish(c, acc):
-            cols = slice(c * CHUNK, (c + 1) * CHUNK)
-            y = keep.tile([P, PACK, CHUNK], F32, name="y%d" % c)
+        def activate(c, acc, y):
             for u in range(PACK):
                 nc.scalar.activation(y[:, u, :], acc[u], SILU, bias=bias[:, u : u + 1])
-            nc.sync.dma_start(out=out_rows[:, :, cols], in_=y[:])
-            y_grouped = keep.tile([P, CHUNK, PACK], BF16, name="y_grouped%d" % c, align_bytes=64)
+            nc.sync.dma_start(out=out_rows[:, :, c * CHUNK : (c + 1) * CHUNK], in_=y)
+
+        def hand_on(first, y, slot):
+            width = y.shape[2]
+            cols = slice(first * CHUNK, first * CHUNK + width)
+            y_grouped = keep.tile([P, width, PACK], BF16, name="y_grouped%d" % first, tag=slot, align_bytes=64)
             nc.vector.tensor_copy(
-                y_grouped[:].rearrange("p (g i) u -> p g u i", i=4), y[:].rearrange("p u (g i) -> p g u i", i=4)
+                y_grouped[:].rearrange("p (g i) u -> p g u i", i=4), y.rearrange("p u (g i) -> p g u i", i=4)
             )
             nc.vector.quantize_mx(
                 out=y_codes[:, cols].bitcast(FP8X4),
@@ -172,18 +173,25 @@ def tile_attend_plh_bsilu_kernel(tc, qT, k_words, k_scales, nb, offs, out_0, out
                 in_=y_grouped[:].rearrange("p q u -> p (q u)"),
             )
 
-        accs = {}
-        for step in range(CHUNKS + 1):
-            if step < CHUNKS:
-                accs[step] = multiply(step, *quantise_queries(step))
-            if step >= 1:
-                finish(step - 1, accs[step - 1])
-            if step >= CHUNKS - 1:
-                cols = slice(0, step * CHUNK) if step < CHUNKS else slice((step - 1) * CHUNK, QUERIES)
-                nc.sync.dma_start(out=out_words[:, cols], in_=y_codes[:, cols].bitcast(I32))
+        quantised = [quantise_queries(0)]
+        load_queries(2)
+        load_queries(3)
+        for c in range(1, CHUNKS):
+            quantised.append(quantise_queries(c))
+        accs = [multiply(c, *quantised[c]) for c in range(CHUNKS)]
+        y_front = keep.tile([P, PACK, 2 * CHUNK], F32, name="y_front", tag="slot0", align_bytes=64)
+        activate(0, accs[0], y_front[:, :, 0:CHUNK])
+        activate(1, accs[1], y_front[:, :, CHUNK : 2 * CHUNK])
+        hand_on(0, y_front[:], "slot5")
+        nc.sync.dma_start(out=out_words[:, 0 : 2 * CHUNK], in_=y_codes[:, 0 : 2 * CHUNK].bitcast(I32))
+        for c in (2, 3):
+            y = keep.tile([P, PACK, CHUNK], F32, name="y%d" % c)
+            activate(c, accs[c], y[:])
+            hand_on(c, y[:], "y_grouped%d" % c)
+        nc.scalar.dma_start(out=out_words[:, 2 * CHUNK : QUERIES], in_=y_codes[:, 2 * CHUNK : QUERIES].bitcast(I32))
 
         for quad in range(4):
-            queue = nc.scalar if quad % 2 == 0 else nc.sync
+            queue = nc.scalar if quad == 3 else nc.sync
             queue.dma_start(
                 out=out_2[0, PACK * quad : PACK * (quad + 1), :].bitcast(I32),
                 in_=y_plane[QUAD * quad : QUAD * quad + PACK, :].bitcast(I32),

@@ -19,10 +19,13 @@ PASSES = 2
 SLOTS = 512
 POOL = 2048
 QUERIES = 512
+HALF = QUERIES // 2
 CHUNK = 128
 CHUNKS = QUERIES // CHUNK
 QUAD = 32
 LIVE = 3 * QUAD + PACK
+RUN = 4
+VECTOR_ZEROES = ((0, 383), (383, 768), (768, 959), (959, 1152))
 FLOPS = 2 * SLOTS * PASSES * P * PACK * QUERIES
 
 
@@ -37,22 +40,23 @@ def tile_attend_plh_bsilu_kernel(tc, qT, k_words, k_scales, nb, offs, out_0, out
 
         bias_window = keep.tile([P, POOL], F32, name="bias_window", tag="slot1", align_bytes=64)
         nc.sync.dma_start(out=bias_window[P - 1 : P, :], in_=nb[0:1, :])
-        q_rows = qT[0].rearrange("(o p j) q -> p j o q", o=PASSES, j=PACK)
-        raws = {}
+        q_rows = qT[0].rearrange("(o p j) q -> o p j q", o=PASSES, j=PACK)
 
-        def load_queries(c):
-            raw = keep.tile([P, PACK, PASSES, CHUNK], F32, name="raw%d" % c, tag="slot%d" % (0, 1, 0, 3)[c], align_bytes=64)
-            nc.sync.dma_start(out=raw[:], in_=q_rows[:, :, :, c * CHUNK : (c + 1) * CHUNK])
-            raws[c] = raw
+        def load_queries(o, first, width, slot):
+            raw = keep.tile([P, PACK, width], F32, name="raw%d_%d" % (o, first), tag=slot, align_bytes=64)
+            nc.sync.dma_start(out=raw[:], in_=q_rows[o][:, :, first : first + width])
+            return raw
 
-        load_queries(0)
+        raw_a = load_queries(0, 0, HALF, "slot0")
+
         scale_window = keep.tile([P, POOL], U8, name="scale_window", tag="slot6", align_bytes=64)
         nc.gpsimd.memset(scale_window[:].bitcast(I32), 0)
-        for quad in range(4):
+        for quad in range(P // QUAD):
             nc.sync.dma_start(
                 out=scale_window[QUAD * quad : QUAD * quad + PASSES * PACK, :].bitcast(I32),
                 in_=k_scales[:, PACK * quad : PACK * (quad + 1), :].bitcast(I32),
             )
+
         seed = keep.tile([P, 8], F32, name="seed", tag="slot4", align_bytes=64)
         nc.gpsimd.memset(seed[:], 0.0)
         warm_in = keep.tile([P, 8], BF16, name="warm_in")
@@ -64,9 +68,10 @@ def tile_attend_plh_bsilu_kernel(tc, qT, k_words, k_scales, nb, offs, out_0, out
             out=word_window[:].bitcast(I32),
             in_=k_words[0].rearrange("p t b -> p (t b)").bitcast(I32),
         )
-        for start, stop in ((0, 383), (383, 768), (768, 959), (959, 1152)):
+
+        for start, stop in VECTOR_ZEROES:
             nc.vector.memset(bias_window[0 : P - 1, start:stop], 0.0)
-        nc.gpsimd.memset(bias_window[0 : P - 1, 1152:POOL], 0.0)
+        nc.gpsimd.memset(bias_window[0 : P - 1, VECTOR_ZEROES[-1][1] : POOL], 0.0)
         second_plane = keep.tile([P, SLOTS], U8, name="second_plane", align_bytes=64)
         nc.vector.memset(second_plane[:].bitcast(I32), 0)
         identity = keep.tile([P, P], F32, name="identity")
@@ -74,14 +79,14 @@ def tile_attend_plh_bsilu_kernel(tc, qT, k_words, k_scales, nb, offs, out_0, out
 
         bias_listed = keep.tile([P, SLOTS], F32, name="bias_listed", align_bytes=64)
         nc.vector.tensor_copy(bias_listed[:], bias_window[:].indirect(offsets[:]))
-        load_queries(1)
+        raw_b = load_queries(1, 0, HALF, "slot1")
         bias_turned = psum.tile([P, PACK, P], F32, name="bias_turned", tag="bank7")
         for u in range(PACK):
             nc.tensor.transpose(bias_turned[:, u, :], bias_listed[:, u:SLOTS:PACK], identity[:])
         bias = keep.tile([P, PACK], F32, name="bias")
         nc.scalar.copy(bias[:], bias_turned[:, :, P - 1])
 
-        scales_listed = keep.tile([P, SLOTS], U8, name="scales_listed", align_bytes=64)
+        scales_listed = keep.tile([P, SLOTS], U8, name="scales_listed", tag="slot2", align_bytes=64)
         nc.vector.tensor_copy(scales_listed[:], scale_window[:].indirect(offsets[:]))
         scales_dealt = keep.tile([P, SLOTS], U8, name="scales_dealt", align_bytes=64)
         nc.vector.tensor_copy(
@@ -107,52 +112,50 @@ def tile_attend_plh_bsilu_kernel(tc, qT, k_words, k_scales, nb, offs, out_0, out
         out_rows = out_0.rearrange("(p u) q -> p u q", u=PACK)
         out_words = out_1[0].rearrange("p q b -> p (q b)").bitcast(I32)
 
-        def quantise_queries(c):
-            grouped = keep.tile(
-                [P, PASSES, CHUNK, PACK], BF16, name="grouped%d" % c, tag="slot%d" % (3, 5, 4, 5)[c], align_bytes=64
-            )
-            source = raws[c][:].rearrange("p j o (g i) -> p o g j i", i=4)
-            target = grouped[:].rearrange("p o (g i) j -> p o g j i", i=4)
-            if c < 2:
-                nc.scalar.copy(target, source)
-            elif c == 2:
-                nc.scalar.copy(target[:, 0], source[:, 0])
-                nc.vector.tensor_copy(target[:, 1], source[:, 1])
-            else:
-                nc.vector.tensor_copy(target, source)
-            codes = keep.tile([P, PASSES, CHUNK], U32, name="q_codes%d" % c, tag="slot%d" % (6, 7, 8, 9)[c], align_bytes=64)
-            plane = keep.tile([P, PASSES, CHUNK], U8, name="q_plane%d" % c, align_bytes=64)
-            nc.vector.quantize_mx(
-                out=codes[:].rearrange("p o q -> p (o q)").bitcast(FP8X4),
-                scales=plane[:].rearrange("p o q -> p (o q)"),
-                in_=grouped[:].rearrange("p o q j -> p (o q j)"),
-            )
-            return codes, plane
+        def quantise_queries(casts, calls, grouped_slot, codes_slot, label):
+            grouped = keep.tile([P, HALF, PACK], BF16, name="grouped_" + label, tag=grouped_slot, align_bytes=64)
+            cast_width = HALF // len(casts)
+            for n, (cast, raw) in enumerate(casts):
+                cols = slice(n * cast_width, (n + 1) * cast_width)
+                cast(
+                    grouped[:, cols, :].rearrange("p (g i) j -> p g j i", i=RUN),
+                    raw.rearrange("p j (g i) -> p g j i", i=RUN),
+                )
+            codes = keep.tile([P, HALF], U32, name="codes_" + label, tag=codes_slot, align_bytes=64)
+            plane = keep.tile([P, HALF], U8, name="plane_" + label, align_bytes=64)
+            call_width = HALF // calls
+            for n in range(calls):
+                cols = slice(n * call_width, (n + 1) * call_width)
+                nc.vector.quantize_mx(
+                    out=codes[:, cols].bitcast(FP8X4),
+                    scales=plane[:, cols],
+                    in_=grouped[:, cols, :].rearrange("p q j -> p (q j)"),
+                )
+            return [(codes[:, first : first + CHUNK], plane[:, first : first + CHUNK]) for first in (0, CHUNK)]
 
-        def multiply(c, codes, plane):
-            banks = (4, 1, 1, 2)[c]
-            first = (0, 4, 5, 6)[c]
+        def multiply(c, first_bank, banks, pass_order):
             share = PACK // banks
             tiles = [
-                psum.tile([P, share, CHUNK], F32, name="acc%d_%d" % (c, b), tag="bank%d" % (first + b)) for b in range(banks)
+                psum.tile([P, share, CHUNK], F32, name="acc%d_%d" % (c, b), tag="bank%d" % (first_bank + b))
+                for b in range(banks)
             ]
             acc = [tiles[u // share][:, u % share, :] for u in range(PACK)]
-            if c == 0:
-                order = [(u, o) for o in (0, 1) for u in range(PACK)]
+            if share == 1:
+                order = [(u, o) for o in pass_order for u in range(PACK)]
             else:
-                order = [(u, o) for u in range(PACK) for o in (1, 0)]
+                order = [(u, o) for u in range(PACK) for o in pass_order]
             for u, o in order:
-                if True:
-                    column = (o * PACK + u) * P
-                    nc.tensor.matmul_mx(
-                        out=acc[u],
-                        lhsT=k_codes[:, 2 * column : 2 * (column + P)].bitcast(FP4X4),
-                        lhsT_scale=k_planes[o][:, u * P : (u + 1) * P],
-                        rhs=codes[:, o, :].bitcast(FP8X4),
-                        rhs_scale=plane[:, o, :],
-                        start=(o == order[0][1]),
-                        stop=(o != order[0][1]),
-                    )
+                column = (o * PACK + u) * P
+                codes, plane = moving[o][c]
+                nc.tensor.matmul_mx(
+                    out=acc[u],
+                    lhsT=k_codes[:, 2 * column : 2 * (column + P)].bitcast(FP4X4),
+                    lhsT_scale=k_planes[o][:, u * P : (u + 1) * P],
+                    rhs=codes.bitcast(FP8X4),
+                    rhs_scale=plane,
+                    start=(o == pass_order[0]),
+                    stop=(o == pass_order[1]),
+                )
             return acc
 
         def activate(c, acc, y):
@@ -160,12 +163,12 @@ def tile_attend_plh_bsilu_kernel(tc, qT, k_words, k_scales, nb, offs, out_0, out
                 nc.scalar.activation(y[:, u, :], acc[u], SILU, bias=bias[:, u : u + 1])
             nc.sync.dma_start(out=out_rows[:, :, c * CHUNK : (c + 1) * CHUNK], in_=y)
 
-        def hand_on(first, y, slot):
+        def hand_on(c, y, slot):
             width = y.shape[2]
-            cols = slice(first * CHUNK, first * CHUNK + width)
-            y_grouped = keep.tile([P, width, PACK], BF16, name="y_grouped%d" % first, tag=slot, align_bytes=64)
+            cols = slice(c * CHUNK, c * CHUNK + width)
+            y_grouped = keep.tile([P, width, PACK], BF16, name="y_grouped%d" % c, tag=slot, align_bytes=64)
             nc.vector.tensor_copy(
-                y_grouped[:].rearrange("p (g i) u -> p g u i", i=4), y.rearrange("p u (g i) -> p g u i", i=4)
+                y_grouped[:].rearrange("p (g i) u -> p g u i", i=RUN), y.rearrange("p u (g i) -> p g u i", i=RUN)
             )
             nc.vector.quantize_mx(
                 out=y_codes[:, cols].bitcast(FP8X4),
@@ -173,25 +176,33 @@ def tile_attend_plh_bsilu_kernel(tc, qT, k_words, k_scales, nb, offs, out_0, out
                 in_=y_grouped[:].rearrange("p q u -> p (q u)"),
             )
 
-        quantised = [quantise_queries(0)]
-        load_queries(2)
-        load_queries(3)
-        for c in range(1, CHUNKS):
-            quantised.append(quantise_queries(c))
-        accs = [multiply(c, *quantised[c]) for c in range(CHUNKS)]
-        y_front = keep.tile([P, PACK, 2 * CHUNK], F32, name="y_front", tag="slot0", align_bytes=64)
+        on_scalar, on_vector = nc.scalar.copy, nc.vector.tensor_copy
+        moving_a = quantise_queries([(on_scalar, raw_a[:])], 1, "slot3", "slot6", "a")
+        raw_c = load_queries(1, HALF, HALF, "slot0")
+        raw_d = load_queries(0, HALF, CHUNK, "slot2")
+        raw_e = load_queries(0, HALF + CHUNK, CHUNK, "slot3")
+        moving_b = quantise_queries([(on_scalar, raw_b[:])], 1, "slot5", "slot7", "b")
+        moving_c = quantise_queries(
+            [(on_scalar, raw_c[:, :, 0:CHUNK]), (on_vector, raw_c[:, :, CHUNK:HALF])], 1, "slot4", "codes_c", "c"
+        )
+        moving_d = quantise_queries([(on_vector, raw_d[:]), (on_vector, raw_e[:])], 2, "slot5", "codes_d", "d")
+        moving = [moving_a + moving_d, moving_b + moving_c]
+
+        accs = [multiply(0, 0, 4, (0, 1)), multiply(1, 4, 2, (1, 0)), multiply(2, 6, 2, (1, 0))]
+        y_front = keep.tile([P, PACK, HALF], F32, name="y_front", tag="slot0", align_bytes=64)
         activate(0, accs[0], y_front[:, :, 0:CHUNK])
-        activate(1, accs[1], y_front[:, :, CHUNK : 2 * CHUNK])
+        accs.append(multiply(3, 0, 4, (1, 0)))
+        activate(1, accs[1], y_front[:, :, CHUNK:HALF])
         hand_on(0, y_front[:], "slot5")
-        nc.sync.dma_start(out=out_words[:, 0 : 2 * CHUNK], in_=y_codes[:, 0 : 2 * CHUNK].bitcast(I32))
-        for c in (2, 3):
+        nc.sync.dma_start(out=out_words[:, 0:HALF], in_=y_codes[:, 0:HALF].bitcast(I32))
+        for c in range(CHUNKS // 2, CHUNKS):
             y = keep.tile([P, PACK, CHUNK], F32, name="y%d" % c)
             activate(c, accs[c], y[:])
             hand_on(c, y[:], "y_grouped%d" % c)
-        nc.scalar.dma_start(out=out_words[:, 2 * CHUNK : QUERIES], in_=y_codes[:, 2 * CHUNK : QUERIES].bitcast(I32))
 
-        for quad in range(4):
-            queue = nc.scalar if quad == 3 else nc.sync
+        nc.scalar.dma_start(out=out_words[:, HALF:QUERIES], in_=y_codes[:, HALF:QUERIES].bitcast(I32))
+        for quad in range(P // QUAD):
+            queue = nc.scalar if quad == P // QUAD - 1 else nc.sync
             queue.dma_start(
                 out=out_2[0, PACK * quad : PACK * (quad + 1), :].bitcast(I32),
                 in_=y_plane[QUAD * quad : QUAD * quad + PACK, :].bitcast(I32),

from contextlib import ExitStack

import concourse.mybir as mybir
from concourse.masks import make_identity

F32 = mybir.dt.float32
BF16 = mybir.dt.bfloat16
I32 = mybir.dt.int32
U32 = mybir.dt.uint32
U16 = mybir.dt.uint16
U8 = mybir.dt.uint8
FP8X4 = mybir.dt.float8_e4m3fn_x4
FP4X4 = mybir.dt.float4_e2m1fn_x4
SILU = mybir.ActivationFunctionType.Silu

P = 128
PACK = 4
PASSES = 2
SLOTS = 512
POOL = 2048
QUERIES = 512
HALF = QUERIES // 2
CHUNK = 128
CHUNKS = QUERIES // CHUNK
QUAD = 32
LIVE = 3 * QUAD + PACK
RUN = 4
VECTOR_ZEROES = ((0, 383), (383, 768), (768, 959), (959, 1152))
FLOPS = 2 * SLOTS * PASSES * P * PACK * QUERIES


def tile_attend_plh_bsilu_kernel(tc, qT, k_words, k_scales, nb, offs, out_0, out_1, out_2):
    nc = tc.nc
    with ExitStack() as ctx:
        keep = ctx.enter_context(tc.tile_pool(name="keep", bufs=1))
        psum = ctx.enter_context(tc.psum_pool(name="psum", bufs=1))

        offsets = keep.tile([P, SLOTS // 16], U16, name="offsets")
        nc.sync.dma_start(offsets[:], offs)

        bias_window = keep.tile([P, POOL], F32, name="bias_window", tag="slot1", align_bytes=64)
        nc.sync.dma_start(out=bias_window[P - 1 : P, :], in_=nb[0:1, :])
        q_rows = qT[0].rearrange("(o p j) q -> o p j q", o=PASSES, j=PACK)

        def load_queries(o, first, width, slot):
            raw = keep.tile([P, PACK, width], F32, name="raw%d_%d" % (o, first), tag=slot, align_bytes=64)
            nc.sync.dma_start(out=raw[:], in_=q_rows[o][:, :, first : first + width])
            return raw

        raw_a = load_queries(0, 0, HALF, "slot0")

        scale_window = keep.tile([P, POOL], U8, name="scale_window", tag="slot6", align_bytes=64)
        nc.gpsimd.memset(scale_window[:].bitcast(I32), 0)
        for quad in range(P // QUAD):
            nc.sync.dma_start(
                out=scale_window[QUAD * quad : QUAD * quad + PASSES * PACK, :].bitcast(I32),
                in_=k_scales[:, PACK * quad : PACK * (quad + 1), :].bitcast(I32),
            )

        seed = keep.tile([P, 8], F32, name="seed", tag="slot4", align_bytes=64)
        nc.gpsimd.memset(seed[:], 0.0)
        warm_in = keep.tile([P, 8], BF16, name="warm_in")
        nc.vector.tensor_copy(warm_in[:], seed[:])
        warm_out = keep.tile([P, 8], F32, name="warm_out")
        nc.scalar.activation(warm_out[:], warm_in[:], SILU)
        word_window = keep.tile([P, POOL], U32, name="word_window", tag="slot4", align_bytes=64)
        nc.sync.dma_start(
            out=word_window[:].bitcast(I32),
            in_=k_words[0].rearrange("p t b -> p (t b)").bitcast(I32),
        )

        for start, stop in VECTOR_ZEROES:
            nc.vector.memset(bias_window[0 : P - 1, start:stop], 0.0)
        nc.gpsimd.memset(bias_window[0 : P - 1, VECTOR_ZEROES[-1][1] : POOL], 0.0)
        second_plane = keep.tile([P, SLOTS], U8, name="second_plane", align_bytes=64)
        nc.vector.memset(second_plane[:].bitcast(I32), 0)
        identity = keep.tile([P, P], F32, name="identity")
        make_identity(nc, identity[:])

        bias_listed = keep.tile([P, SLOTS], F32, name="bias_listed", align_bytes=64)
        nc.vector.tensor_copy(bias_listed[:], bias_window[:].indirect(offsets[:]))
        raw_b = load_queries(1, 0, HALF, "slot1")
        bias_turned = psum.tile([P, PACK, P], F32, name="bias_turned", tag="bank7")
        for u in range(PACK):
            nc.tensor.transpose(bias_turned[:, u, :], bias_listed[:, u:SLOTS:PACK], identity[:])
        bias = keep.tile([P, PACK], F32, name="bias")
        nc.scalar.copy(bias[:], bias_turned[:, :, P - 1])

        scales_listed = keep.tile([P, SLOTS], U8, name="scales_listed", tag="slot2", align_bytes=64)
        nc.vector.tensor_copy(scales_listed[:], scale_window[:].indirect(offsets[:]))
        scales_dealt = keep.tile([P, SLOTS], U8, name="scales_dealt", align_bytes=64)
        nc.vector.tensor_copy(
            scales_dealt[:].rearrange("p (u h l) -> p h u l", u=PACK, l=4),
            scales_listed[:].rearrange("p (h l u) -> p h u l", u=PACK, l=4),
        )
        nc.sync.dma_start(
            out=second_plane[0:LIVE, :].bitcast(I32),
            in_=scales_dealt[PACK : PACK + LIVE, :].bitcast(I32),
        )
        k_planes = [scales_dealt, second_plane]

        words_listed = keep.tile([P, SLOTS], U32, name="words_listed", tag="slot7", align_bytes=64)
        nc.vector.tensor_copy(words_listed[:], word_window[:].indirect(offsets[:]))
        k_codes = keep.tile([P, PASSES * SLOTS * 2], U8, name="k_codes", align_bytes=64)
        nc.vector.tensor_copy(
            k_codes[:].bitcast(U16).rearrange("p (o u h l) -> p o h u l", o=PASSES, u=PACK, l=2),
            words_listed[:].bitcast(U16).rearrange("p (h l u o) -> p o h u l", o=PASSES, u=PACK, l=2),
        )

        y_codes = keep.tile([P, QUERIES], U32, name="y_codes", align_bytes=64)
        y_plane = keep.tile([P, QUERIES], U8, name="y_plane", align_bytes=64)
        out_rows = out_0.rearrange("(p u) q -> p u q", u=PACK)
        out_words = out_1[0].rearrange("p q b -> p (q b)").bitcast(I32)

        def quantise_queries(casts, calls, grouped_slot, codes_slot, label):
            grouped = keep.tile([P, HALF, PACK], BF16, name="grouped_" + label, tag=grouped_slot, align_bytes=64)
            cast_width = HALF // len(casts)
            for n, (cast, raw) in enumerate(casts):
                cols = slice(n * cast_width, (n + 1) * cast_width)
                cast(
                    grouped[:, cols, :].rearrange("p (g i) j -> p g j i", i=RUN),
                    raw.rearrange("p j (g i) -> p g j i", i=RUN),
                )
            codes = keep.tile([P, HALF], U32, name="codes_" + label, tag=codes_slot, align_bytes=64)
            plane = keep.tile([P, HALF], U8, name="plane_" + label, align_bytes=64)
            call_width = HALF // calls
            for n in range(calls):
                cols = slice(n * call_width, (n + 1) * call_width)
                nc.vector.quantize_mx(
                    out=codes[:, cols].bitcast(FP8X4),
                    scales=plane[:, cols],
                    in_=grouped[:, cols, :].rearrange("p q j -> p (q j)"),
                )
            return [(codes[:, first : first + CHUNK], plane[:, first : first + CHUNK]) for first in (0, CHUNK)]

        def multiply(c, first_bank, banks, pass_order):
            share = PACK // banks
            tiles = [
                psum.tile([P, share, CHUNK], F32, name="acc%d_%d" % (c, b), tag="bank%d" % (first_bank + b))
                for b in range(banks)
            ]
            acc = [tiles[u // share][:, u % share, :] for u in range(PACK)]
            if share == 1:
                order = [(u, o) for o in pass_order for u in range(PACK)]
            else:
                order = [(u, o) for u in range(PACK) for o in pass_order]
            for u, o in order:
                column = (o * PACK + u) * P
                codes, plane = moving[o][c]
                nc.tensor.matmul_mx(
                    out=acc[u],
                    lhsT=k_codes[:, 2 * column : 2 * (column + P)].bitcast(FP4X4),
                    lhsT_scale=k_planes[o][:, u * P : (u + 1) * P],
                    rhs=codes.bitcast(FP8X4),
                    rhs_scale=plane,
                    start=(o == pass_order[0]),
                    stop=(o == pass_order[1]),
                )
            return acc

        def activate(c, acc, y):
            for u in range(PACK):
                nc.scalar.activation(y[:, u, :], acc[u], SILU, bias=bias[:, u : u + 1])
            nc.sync.dma_start(out=out_rows[:, :, c * CHUNK : (c + 1) * CHUNK], in_=y)

        def hand_on(c, y, slot):
            width = y.shape[2]
            cols = slice(c * CHUNK, c * CHUNK + width)
            y_grouped = keep.tile([P, width, PACK], BF16, name="y_grouped%d" % c, tag=slot, align_bytes=64)
            nc.vector.tensor_copy(
                y_grouped[:].rearrange("p (g i) u -> p g u i", i=RUN), y.rearrange("p u (g i) -> p g u i", i=RUN)
            )
            nc.vector.quantize_mx(
                out=y_codes[:, cols].bitcast(FP8X4),
                scales=y_plane[:, cols],
                in_=y_grouped[:].rearrange("p q u -> p (q u)"),
            )

        on_scalar, on_vector = nc.scalar.copy, nc.vector.tensor_copy
        moving_a = quantise_queries([(on_scalar, raw_a[:])], 1, "slot3", "slot6", "a")
        raw_c = load_queries(1, HALF, HALF, "slot0")
        raw_d = load_queries(0, HALF, CHUNK, "slot2")
        raw_e = load_queries(0, HALF + CHUNK, CHUNK, "slot3")
        moving_b = quantise_queries([(on_scalar, raw_b[:])], 1, "slot5", "slot7", "b")
        moving_c = quantise_queries(
            [(on_scalar, raw_c[:, :, 0:CHUNK]), (on_vector, raw_c[:, :, CHUNK:HALF])], 1, "slot4", "codes_c", "c"
        )
        moving_d = quantise_queries([(on_vector, raw_d[:]), (on_vector, raw_e[:])], 2, "slot5", "codes_d", "d")
        moving = [moving_a + moving_d, moving_b + moving_c]

        accs = [multiply(0, 0, 4, (0, 1)), multiply(1, 4, 2, (1, 0)), multiply(2, 6, 2, (1, 0))]
        y_front = keep.tile([P, PACK, HALF], F32, name="y_front", tag="slot0", align_bytes=64)
        activate(0, accs[0], y_front[:, :, 0:CHUNK])
        accs.append(multiply(3, 0, 4, (1, 0)))
        activate(1, accs[1], y_front[:, :, CHUNK:HALF])
        hand_on(0, y_front[:], "slot5")
        nc.sync.dma_start(out=out_words[:, 0:HALF], in_=y_codes[:, 0:HALF].bitcast(I32))
        for c in range(CHUNKS // 2, CHUNKS):
            y = keep.tile([P, PACK, CHUNK], F32, name="y%d" % c)
            activate(c, accs[c], y[:])
            hand_on(c, y[:], "y_grouped%d" % c)

        nc.scalar.dma_start(out=out_words[:, HALF:QUERIES], in_=y_codes[:, HALF:QUERIES].bitcast(I32))
        for quad in range(P // QUAD):
            queue = nc.scalar if quad == P // QUAD - 1 else nc.sync
            queue.dma_start(
                out=out_2[0, PACK * quad : PACK * (quad + 1), :].bitcast(I32),
                in_=y_plane[QUAD * quad : QUAD * quad + PACK, :].bitcast(I32),
            )
